import numpy as np
import ml_dtypes


def mxq(x, axis, fmt="e4m3"):
    dtype, down = {"e4m3": (ml_dtypes.float8_e4m3fn, 7), "e5m2": (ml_dtypes.float8_e5m2, 14)}[fmt]
    v = np.moveaxis(np.asarray(x, np.float32).astype(ml_dtypes.bfloat16).astype(np.float64), axis, -1)
    blocks = v.reshape(v.shape[:-1] + (-1, 32))
    amax = np.abs(blocks).max(-1, keepdims=True)
    byte = np.maximum(np.where(amax > 0, np.frexp(amax)[1] - 1 + 127, 0) - down, 1)
    scale = np.exp2(byte - 127.0)
    codes = (blocks / scale).astype(np.float32).astype(dtype).astype(np.float64)
    return np.moveaxis((codes * scale).reshape(v.shape), -1, axis)


WIDE = False


def mx_kscale(k):
    if not WIDE:
        return np.ones(k)
    levels = np.array([10, -10, 5, -5, 0])
    if k % 512:
        return np.exp2(np.random.permutation(np.resize(levels, k // 32))).repeat(32)
    a = np.empty((k // 512, 16))
    for p in range(k // 512):
        a[p, :8] = np.random.permutation(np.resize(levels, 8))
        for g in range(8):
            far = levels[np.abs(levels - a[p, g]) >= 10]
            a[p, g + 8] = far[np.random.randint(len(far))]
    return np.exp2(a.ravel()).repeat(32)


def f64(x):
    return np.asarray(x).astype(np.float64)


def striped(idx):
    return np.tile(idx.reshape(-1, 16).T, (8, 1)).astype(np.uint16)


def unstriped(offs):
    return offs[:16].T.reshape(-1).astype(np.int64)


E2M1 = np.array([0.0, 0.5, 1.0, 1.5, 2.0, 3.0, 4.0, 6.0, -0.0, -0.5, -1.0, -1.5, -2.0, -3.0, -4.0, -6.0])


def pack_weight(w, fmt):
    k, n = w.shape
    w = f64(np.asarray(w, np.float32).astype(ml_dtypes.bfloat16)).reshape(k // 32, 32, n)
    amax = np.abs(w).max(1)
    if fmt == "e4m3":
        byte = np.frexp(amax)[1] - 1 + 127 - 7
    else:
        mant, ex = np.frexp(amax / 6.0)
        byte = np.where(mant > 0.5, ex, ex - 1) + 127
    byte = np.clip(np.where(amax > 0, byte, 1), 1, 254)
    scaled = (w * np.exp2(127.0 - byte)[:, None, :]).reshape(k, n).astype(np.float32)
    by_word = np.ascontiguousarray(scaled.reshape(k // 512, 128, 4, n).transpose(0, 1, 3, 2))
    if fmt == "e4m3":
        words = by_word.astype(ml_dtypes.float8_e4m3fn).view(np.uint8)
    else:
        c = by_word.astype(ml_dtypes.float4_e2m1fn).view(np.uint8) & 0xF
        words = (c[..., 0::2] | (c[..., 1::2] << 4)).reshape(k // 512, 128, 2 * n)
    return np.ascontiguousarray(words), np.ascontiguousarray(byte.astype(np.uint8).reshape(k // 512, 16, n))


def unpack_weight(words, scales, fmt):
    g, _, n = scales.shape
    words = np.ascontiguousarray(words).reshape(g, 128, n, -1)
    if fmt == "e4m3":
        vals = words.view(ml_dtypes.float8_e4m3fn).astype(np.float64)
    else:
        nib = np.empty((g, 128, n, 4), np.uint8)
        nib[..., 0::2] = words & 0xF
        nib[..., 1::2] = words >> 4
        vals = E2M1[nib]
    vals = vals * np.repeat(np.exp2(scales.astype(np.float64) - 127.0), 8, axis=1)[..., None]
    return vals.transpose(0, 1, 3, 2).reshape(g * 512, n)


def gelu(v):
    return 0.5 * v * (1.0 + np.tanh(np.sqrt(2.0 / np.pi) * (v + 0.044715 * v**3)))


def striped8(idx):
    return np.concatenate([v.reshape(-1, 16).T for v in idx]).astype(np.uint16)


def unstriped8(offs):
    return np.stack([offs[16 * g:16 * g + 16].T.reshape(-1) for g in range(8)]).astype(np.int64)


def heads(h, wgt, idx8):
    r = np.arange(h.shape[0])
    return wgt[r // 4 % 128] * h[r[:, None], idx8[r % 512 // 64]]


def bf(x):
    return np.asarray(x, np.float32).astype(ml_dtypes.bfloat16)


def planes(Y):
    n, m = Y.shape
    b = f64(bf(Y)).reshape(n // 32, 32, m)
    amax = np.abs(b).max(1)
    byte = np.clip(np.where(amax > 0, np.frexp(amax)[1] - 1 + 127 - 7, 1), 1, 254)
    codes = (b * np.exp2(127.0 - byte)[:, None, :]).reshape(n, m).astype(np.float32).astype(ml_dtypes.float8_e4m3fn).view(np.uint8)
    words = codes.reshape(n // 512, 128, 4, m).transpose(0, 1, 3, 2)
    return np.ascontiguousarray(words), np.ascontiguousarray(byte.astype(np.uint8).reshape(n // 512, 16, m))


K, T, S, H, T2, P, N = 1024, 2048, 512, 1024, 1024, 512, 1024


def setup_inputs():
    n = np.random.standard_normal
    s = mx_kscale(K)[:, None]
    u = mx_kscale(H)[:, None]
    tab_words, tab_scales = pack_weight(n((K, T)) * s, "e4m3")
    w1 = n((K, H)) / s / np.sqrt(K)
    gain = np.random.uniform(0.05, 0.19, H) * u[:, 0]
    page0 = np.random.uniform(-1.4, 1.4, (H, T2)) * u
    wgs = np.exp(0.3 * n((128, S)))
    wgt = np.repeat(np.random.uniform(0.5, 2.0, (8, P)), 16, axis=0)
    freq = np.random.uniform(0.5, 1.0, H) / u[:, 0]
    amp = np.random.uniform(1.2, 2.4, H) * u[:, 0]
    w2 = 0.5 * n((H, N)) / u / np.sqrt(H) * np.exp(0.8 * n(N))
    w2_words, w2_scales = pack_weight(w2, "e2m1")
    return {"tab_words": tab_words, "tab_scales": tab_scales,
            "offs": striped(np.random.permutation(T)[:S]),
            "offs2": striped(np.random.permutation(T2)[:S]),
            "offs3": striped8(np.stack([np.random.permutation(T2)[:P] for _ in range(8)])),
            "w1": w1.astype(np.float32), "gain": gain.astype(np.float32),
            "page0": page0.astype(np.float32), "wgs": wgs.astype(np.float32),
            "wgt": wgt.astype(np.float32), "freq": freq.astype(np.float32),
            "amp": amp.astype(np.float32),
            "w2_words": w2_words, "w2_scales": w2_scales}


def reference(tab_words, tab_scales, offs, offs2, offs3, w1, gain, page0, wgs, wgt, freq, amp, w2_words, w2_scales):
    v = unpack_weight(tab_words, tab_scales, "e4m3")[:, unstriped(offs)]
    h = f64(gain)[:, None] * (mxq(f64(w1), 0, "e4m3").T @ v)
    page = f64(page0).copy()
    page[:, unstriped(offs2)] = np.tile(f64(wgs), (H // 128, 1)) * h
    x = heads(page, f64(wgt), unstriped8(offs3))
    z = x + f64(amp)[:, None] * np.sin(f64(freq)[:, None] * x)
    w2 = unpack_weight(w2_words, w2_scales, "e2m1")
    y = w2.T @ mxq(z, 0, "e4m3")
    words, scales = planes(y)
    return y, words, scales

@@ -1,0 +1,292 @@
+from contextlib import ExitStack
+
+import concourse.mybir as mybir
+
+K, T, S, H, T2, M, N = 1024, 2048, 512, 1024, 1024, 512, 1024
+FLOPS = 2 * K * H * S + 2 * H * N * M
+
+F32 = mybir.dt.float32
+BF16 = mybir.dt.bfloat16
+I32 = mybir.dt.int32
+U32 = mybir.dt.uint32
+U16 = mybir.dt.uint16
+U8 = mybir.dt.uint8
+FP8X4 = mybir.dt.float8_e4m3fn_x4
+FP4X4 = mybir.dt.float4_e2m1fn_x4
+MULT = mybir.AluOpType.mult
+ADD = mybir.AluOpType.add
+COPY = mybir.ActivationFunctionType.Copy
+SIN = mybir.ActivationFunctionType.Sin
+
+P = 128
+PACK = 4
+PASS = P * PACK
+BANK = 512
+W = 128
+CHUNKS = M // W
+RING = 4
+
+
+def tile_list_channel_resistance_features_kernel(
+    tc, tab_words, tab_scales, offs, offs2, offs3, w1, gain, page0, wgs, wgt, freq, amp,
+    w2_words, w2_scales, out_0, out_1, out_2,
+):
+    nc = tc.nc
+    with ExitStack() as ctx:
+        keep = ctx.enter_context(tc.tile_pool(name="keep", bufs=1))
+        psum = ctx.enter_context(tc.psum_pool(name="psum", bufs=1))
+
+        def tile(name, shape, dtype):
+            return keep.tile(shape, dtype, name=name, align_bytes=64)
+
+        list1 = keep.tile([P, S // 16], U16, name="list1")
+        list2 = keep.tile([P, S // 16], U16, name="list2")
+        list3 = keep.tile([P, M // 16], U16, name="list3")
+        banks = [psum.tile([P, BANK], F32, name="bank%d" % n) for n in range(8)]
+
+        w1_raw = [[tile("w1_raw%d%d" % (a, b), [P, PACK, PASS], F32) for b in range(2)] for a in range(2)]
+        w1_bf = [[tile("w1_bf%d%d" % (a, b), [P, PACK * PASS], BF16) for b in range(2)] for a in range(2)]
+        w1_codes = [[tile("w1_codes%d%d" % (a, b), [P, PASS], U32) for b in range(2)] for a in range(2)]
+        w1_scale = [[tile("w1_scale%d%d" % (a, b), [P, PASS], U8) for b in range(2)] for a in range(2)]
+        tab = [tile("tab%d" % a, [P, T], U32) for a in range(2)]
+        tab_sc = tile("tab_sc", [P, T], U8)
+        v = [tile("v%d" % a, [P, S], U32) for a in range(2)]
+        v_sc = tile("v_sc", [P, S], U8)
+        w2_raw = tile("w2_raw", [P, 4 * N], U8)
+        w2_dealt = tile("w2_dealt", [P, 4 * N], U8)
+        w2_sc_raw = tile("w2_sc_raw", [P, N], U8)
+        w2_sc = [tile("w2_sc%d" % b, [P, N], U8) for b in range(2)]
+        gain_t = tile("gain_t", [P, 8], F32)
+        freq_t = tile("freq_t", [P, 8], F32)
+        amp_t = tile("amp_t", [P, 8], F32)
+        wgs_first = tile("wgs_first", [P, S], F32)
+        wgs_rest = tile("wgs_rest", [P, 3 * S], F32)
+        wgt_t = tile("wgt_t", [P, M], F32)
+        pages = [tile("page%d" % u, [P, T2], F32) for u in range(8)]
+        h = tile("h", [P, 8 * S], F32)
+        x_wide = tile("x_wide", [P, 2 * M], F32)
+        ripple = tile("ripple", [P, 2 * M], F32)
+        y_codes = tile("y_codes", [P, 2 * M], U32)
+        y_scale = tile("y_scale", [P, 2 * M], U8)
+
+        def load_w1(a, b):
+            rows = w1[a * PASS : (a + 1) * PASS, b * PASS : (b + 1) * PASS]
+            nc.sync.dma_start(out=w1_raw[a][b][:], in_=rows.rearrange("(p j) c -> p j c", j=PACK))
+
+        def load_tab(a):
+            nc.sync.dma_start(out=tab[a][:].bitcast(I32), in_=tab_words[a].rearrange("p t i -> p (t i)").bitcast(I32))
+
+        def load_page(u):
+            b, i = divmod(u, PACK)
+            nc.sync.dma_start(out=pages[u][:], in_=page0.rearrange("(b p i) c -> b i p c", b=2, i=PACK)[b, i])
+
+        def load_rows(queue, dst, src):
+            queue.dma_start(
+                out=dst[:].rearrange("p (b i) -> p b i", b=2), in_=src.rearrange("(b p i) -> p b i", b=2, i=PACK)
+            )
+
+        def cast_w1(copy, a, b):
+            copy(
+                out=w1_bf[a][b][:].rearrange("p (i m j) -> p m j i", i=PACK, j=PACK),
+                in_=w1_raw[a][b][:].rearrange("p j (m i) -> p m j i", i=PACK),
+            )
+
+        def quantize(codes, scale, values):
+            nc.vector.quantize_mx(out=codes.bitcast(FP8X4), scales=scale, in_=values)
+
+        nc.gpsimd.memset(tab_sc[:].bitcast(I32), 0)
+        nc.vector.memset(w2_sc_raw[:].bitcast(I32), 0)
+        nc.vector.memset(w2_sc[1][:].bitcast(I32), 0)
+        load_w1(0, 0)
+        for q in range(4):
+            nc.gpsimd.dma_start(
+                out=tab_sc[32 * q : 32 * q + 8, :].bitcast(I32), in_=tab_scales[:, 4 * q : 4 * q + 4, :].bitcast(I32)
+            )
+        for q in range(4):
+            nc.gpsimd.dma_start(
+                out=w2_sc_raw[32 * q : 32 * q + 8, :].bitcast(I32), in_=w2_scales[:, 4 * q : 4 * q + 4, :].bitcast(I32)
+            )
+        load_rows(nc.gpsimd, freq_t, freq)
+        load_rows(nc.gpsimd, amp_t, amp)
+        nc.sync.dma_start(list1[:], offs)
+        nc.sync.dma_start(list2[:], offs2)
+        load_rows(nc.sync, gain_t, gain)
+        load_w1(1, 0)
+        load_tab(0)
+        load_tab(1)
+        nc.sync.dma_start(
+            out=w2_raw[:].bitcast(I32).rearrange("p (b c) -> p b c", b=2),
+            in_=w2_words.bitcast(I32).rearrange("b p c -> p b c"),
+        )
+        load_page(0)
+        wgs_rows = wgs.rearrange("(q i) j -> q i j", i=PACK)
+        for q in range(4):
+            nc.sync.dma_start(out=wgs_first[32 * q : 32 * q + 32, :], in_=wgs_rows[:, 0, :])
+        for q in range(4):
+            nc.sync.dma_start(
+                out=wgs_rest[32 * q : 32 * q + 32, :], in_=wgs_rows[:, 1:PACK, :].rearrange("q i j -> q (i j)")
+            )
+        nc.sync.dma_start(out=wgt_t[:], in_=wgt)
+        nc.sync.dma_start(list3[:], offs3)
+        load_page(1)
+        load_w1(0, 1)
+        load_page(2)
+        load_w1(1, 1)
+        for u in range(3, 8):
+            load_page(u)
+
+        def first_product(u):
+            b, i = divmod(u, PACK)
+            cols = slice(i * P, (i + 1) * P)
+            for a in range(2):
+                nc.tensor.matmul_mx(
+                    out=banks[u][:],
+                    lhsT=w1_codes[a][b][:, cols].bitcast(FP8X4),
+                    lhsT_scale=w1_scale[a][b][:, cols],
+                    rhs=v[a][:].bitcast(FP8X4),
+                    rhs_scale=v_sc[4 * a : P, :],
+                    start=(a == 0),
+                    stop=(a == 1),
+                )
+            nc.scalar.activation(out=h[:, u * S : (u + 1) * S], in_=banks[u][:], func=COPY, scale=gain_t[:, u : u + 1])
+
+        def place(u):
+            i = u % PACK
+            weights = wgs_first[:] if i == 0 else wgs_rest[:, (i - 1) * S : i * S]
+            nc.vector.tensor_tensor(pages[u][:].indirect(list2[:]), h[:, u * S : (u + 1) * S], weights, MULT)
+
+        def deal(dst, src):
+            nc.vector.tensor_copy(
+                out=dst.rearrange("p (a t mb mi) -> p a mb t mi", t=PACK, mb=16, mi=8),
+                in_=src.rearrange("p (a mb mi t) -> p a mb t mi", t=PACK, mb=16, mi=8),
+            )
+
+        z_rows = [h[:, S : 5 * S], tile("z_rows", [P, PACK * M], BF16)[:]]
+        z_bf = [tile("z_bf%d" % b, [P, PACK * M], BF16) for b in range(2)]
+        z_codes = [tile("z_codes%d" % b, [P, M], U32) for b in range(2)]
+        z_scale = [tile("z_scale%d" % b, [P, M], U8) for b in range(2)]
+        y = [[tile("y%d%d" % (c, g), [P, BANK], F32) for g in range(2)] for c in range(CHUNKS)]
+        y_bf = [[tile("y_bf%d%d" % (c, g), [P, BANK], BF16) for g in range(2)] for c in range(CHUNKS)]
+        last = CHUNKS - 1
+
+        def interleave(copy, dst, src):
+            copy(
+                out=dst.rearrange("p (c i t) -> p c t i", i=4, t=PACK),
+                in_=src.rearrange("p (t c i) -> p c t i", i=4, t=PACK),
+            )
+
+        steps = [(u, 0, M) for u in range(PACK)]
+        steps += [(u, c * W, W) for c in range(CHUNKS) for u in range(PACK, 2 * PACK)]
+
+        def buffers(k):
+            u, m0, w = steps[k]
+            if w == M:
+                return x_wide[:, (k % 2) * M : (k % 2 + 1) * M], ripple[:, (k % 2) * M : (k % 2 + 1) * M]
+            slot = k % RING
+            return wgs_rest[:, 2 * S + slot * W : 2 * S + (slot + 1) * W], ripple[:, slot * W : (slot + 1) * W]
+
+        def pick(k):
+            u, m0, w = steps[k]
+            x, s = buffers(k)
+            offsets = list3[:, m0 // 16 : (m0 + w) // 16]
+            nc.vector.tensor_tensor(x, pages[u][:].indirect(offsets), wgt_t[:, m0 : m0 + w], MULT)
+            nc.scalar.activation(out=s, in_=x, func=SIN, scale=freq_t[:, u : u + 1])
+
+        def combine(k):
+            u, m0, w = steps[k]
+            b, i = divmod(u, PACK)
+            x, s = buffers(k)
+            rows = z_rows[b][:, PACK * m0 : PACK * (m0 + w)]
+            nc.vector.scalar_tensor_tensor(
+                out=rows[:, i * w : (i + 1) * w], in0=s, scalar=amp_t[:, u : u + 1], in1=x, op0=MULT, op1=ADD
+            )
+            if i == PACK - 1:
+                copy = nc.vector.tensor_copy if k == len(steps) - 1 else nc.scalar.copy
+                interleave(copy, z_bf[b][:, PACK * m0 : PACK * (m0 + w)], rows)
+
+        def second_product(b, m0, w):
+            quantize(z_codes[b][:, m0 : m0 + w], z_scale[b][:, m0 : m0 + w], z_bf[b][:, PACK * m0 : PACK * (m0 + w)])
+            for c in range(m0 // W, (m0 + w) // W):
+                for n in range(8):
+                    g, t = divmod(n, PACK)
+                    at = b * N + n * P
+                    nc.tensor.matmul_mx(
+                        out=banks[2 * c + g][:, t * W : (t + 1) * W],
+                        lhsT=w2_dealt[:, 2 * at : 2 * (at + P)].bitcast(FP4X4),
+                        lhsT_scale=w2_sc[b][:, n * P : (n + 1) * P],
+                        rhs=z_codes[b][:, c * W : (c + 1) * W].bitcast(FP8X4),
+                        rhs_scale=z_scale[b][:, c * W : (c + 1) * W],
+                        start=(b == 0 and t == 0),
+                        stop=(b == 1 and t == PACK - 1),
+                    )
+
+        def take_out(c, g):
+            on_vector = c == last and g == 1
+            (nc.vector.tensor_copy if on_vector else nc.scalar.copy)(out=y[c][g][:], in_=banks[2 * c + g][:])
+            nc.sync.dma_start(
+                out=out_0.rearrange("(g p t) m -> g p t m", g=2, t=PACK)[g, :, :, c * W : (c + 1) * W],
+                in_=y[c][g][:].rearrange("p (t m) -> p t m", t=PACK),
+            )
+            interleave(nc.vector.tensor_copy if g == 1 else nc.scalar.copy, y_bf[c][g][:], y[c][g][:])
+
+        def planes(c):
+            for g in range(2):
+                cols = slice(g * M + c * W, g * M + (c + 1) * W)
+                quantize(y_codes[:, cols], y_scale[:, cols], y_bf[c][g][:])
+            nc.sync.dma_start(
+                out=out_1.rearrange("g p m t -> p g (m t)").bitcast(I32)[:, :, c * W : (c + 1) * W],
+                in_=y_codes[:].bitcast(I32).rearrange("p (g m) -> p g m", g=2)[:, :, c * W : (c + 1) * W],
+            )
+
+        cast_w1(nc.vector.tensor_copy, 0, 0)
+        nc.vector.tensor_copy(v_sc[:], tab_sc[:].indirect(list1[:]))
+        quantize(w1_codes[0][0][:], w1_scale[0][0][:], w1_bf[0][0][:])
+        cast_w1(nc.scalar.copy, 1, 0)
+        nc.vector.tensor_copy(v[0][:], tab[0][:].indirect(list1[:]))
+        quantize(w1_codes[1][0][:], w1_scale[1][0][:], w1_bf[1][0][:])
+        nc.vector.tensor_copy(v[1][:], tab[1][:].indirect(list1[:]))
+        deal(w2_sc[0][:], w2_sc_raw[:])
+        deal(w2_dealt[:].bitcast(U16), w2_raw[:].bitcast(U16))
+        for u in range(PACK):
+            first_product(u)
+        for u in range(PACK):
+            place(u)
+            if u > 0:
+                combine(u - 1)
+            pick(u)
+            if u in (1, 2):
+                cast_w1(nc.scalar.copy, u - 1, 1)
+                quantize(w1_codes[u - 1][1][:], w1_scale[u - 1][1][:], w1_bf[u - 1][1][:])
+        for q in range(4):
+            nc.gpsimd.dma_start(
+                out=w2_sc[1][32 * q : 32 * q + 4, :].bitcast(I32), in_=w2_sc[0][32 * q + 4 : 32 * q + 8, :].bitcast(I32)
+            )
+        for u in range(PACK, 2 * PACK):
+            first_product(u)
+        place(4)
+        combine(3)
+        place(5)
+        second_product(0, 0, M)
+        place(6)
+        place(7)
+        for k in range(PACK, len(steps) + 8):
+            if k < len(steps):
+                pick(k)
+            if PACK <= k - 1 < len(steps):
+                combine(k - 1)
+            j = k - 3
+            if PACK <= j < len(steps) and j % PACK == PACK - 1:
+                u, m0, w = steps[j]
+                second_product(1, m0, w)
+                take_out(m0 // W, 0)
+                take_out(m0 // W, 1)
+            j = k - 6
+            if PACK <= j < len(steps) and j % PACK == PACK - 1:
+                planes(steps[j][1] // W)
+
+        for q in range(4):
+            queue = nc.sync if q % 2 == 0 else nc.scalar
+            queue.dma_start(
+                out=out_2[:, 4 * q : 4 * q + 4, :].bitcast(I32).rearrange("g r m -> r g m"),
+                in_=y_scale[32 * q : 32 * q + 4, :].bitcast(I32).rearrange("r (g m) -> r g m", g=2),
+            )

@@ -36,8 +36,8 @@ def tile_list_channel_resistance_features_kernel(
         keep = ctx.enter_context(tc.tile_pool(name="keep", bufs=1))
         psum = ctx.enter_context(tc.psum_pool(name="psum", bufs=1))
 
-        def tile(name, shape, dtype):
-            return keep.tile(shape, dtype, name=name, align_bytes=64)
+        def tile(name, shape, dtype, tag=None):
+            return keep.tile(shape, dtype, name=name, tag=tag or name, align_bytes=64)
 
         list1 = keep.tile([P, S // 16], U16, name="list1")
         list2 = keep.tile([P, S // 16], U16, name="list2")
@@ -59,12 +59,12 @@ def tile_list_channel_resistance_features_kernel(
         gain_t = tile("gain_t", [P, 8], F32)
         freq_t = tile("freq_t", [P, 8], F32)
         amp_t = tile("amp_t", [P, 8], F32)
-        wgs_first = tile("wgs_first", [P, S], F32)
+        wgs_first = tile("wgs_first", [P, S], F32, tag="then_page6")
         wgs_rest = tile("wgs_rest", [P, 3 * S], F32)
         wgt_t = tile("wgt_t", [P, M], F32)
-        pages = [tile("page%d" % u, [P, T2], F32) for u in range(8)]
+        x_wide = tile("x_wide", [P, 2 * M], F32, tag="then_page7")
+        pages = [tile("page%d" % u, [P, T2], F32) for u in range(6)]
         h = tile("h", [P, 8 * S], F32)
-        x_wide = tile("x_wide", [P, 2 * M], F32)
         ripple = tile("ripple", [P, 2 * M], F32)
         y_codes = tile("y_codes", [P, 2 * M], U32)
         y_scale = tile("y_scale", [P, 2 * M], U8)
@@ -80,8 +80,8 @@ def tile_list_channel_resistance_features_kernel(
             b, i = divmod(u, PACK)
             nc.sync.dma_start(out=pages[u][:], in_=page0.rearrange("(b p i) c -> b i p c", b=2, i=PACK)[b, i])
 
-        def load_rows(queue, dst, src):
-            queue.dma_start(
+        def load_rows(dst, src):
+            nc.sync.dma_start(
                 out=dst[:].rearrange("p (b i) -> p b i", b=2), in_=src.rearrange("(b p i) -> p b i", b=2, i=PACK)
             )
 
@@ -97,20 +97,14 @@ def tile_list_channel_resistance_features_kernel(
         nc.gpsimd.memset(tab_sc[:].bitcast(I32), 0)
         nc.vector.memset(w2_sc_raw[:].bitcast(I32), 0)
         nc.vector.memset(w2_sc[1][:].bitcast(I32), 0)
-        load_w1(0, 0)
-        for q in range(4):
-            nc.gpsimd.dma_start(
-                out=tab_sc[32 * q : 32 * q + 8, :].bitcast(I32), in_=tab_scales[:, 4 * q : 4 * q + 4, :].bitcast(I32)
-            )
-        for q in range(4):
-            nc.gpsimd.dma_start(
-                out=w2_sc_raw[32 * q : 32 * q + 8, :].bitcast(I32), in_=w2_scales[:, 4 * q : 4 * q + 4, :].bitcast(I32)
-            )
-        load_rows(nc.gpsimd, freq_t, freq)
-        load_rows(nc.gpsimd, amp_t, amp)
         nc.sync.dma_start(list1[:], offs)
         nc.sync.dma_start(list2[:], offs2)
-        load_rows(nc.sync, gain_t, gain)
+        load_rows(gain_t, gain)
+        load_w1(0, 0)
+        for q in range(4):
+            nc.scalar.dma_start(
+                out=tab_sc[32 * q : 32 * q + 8, :].bitcast(I32), in_=tab_scales[:, 4 * q : 4 * q + 4, :].bitcast(I32)
+            )
         load_w1(1, 0)
         load_tab(0)
         load_tab(1)
@@ -128,11 +122,17 @@ def tile_list_channel_resistance_features_kernel(
             )
         nc.sync.dma_start(out=wgt_t[:], in_=wgt)
         nc.sync.dma_start(list3[:], offs3)
+        load_rows(freq_t, freq)
         load_page(1)
+        load_rows(amp_t, amp)
         load_w1(0, 1)
         load_page(2)
         load_w1(1, 1)
-        for u in range(3, 8):
+        for q in range(4):
+            nc.sync.dma_start(
+                out=w2_sc_raw[32 * q : 32 * q + 8, :].bitcast(I32), in_=w2_scales[:, 4 * q : 4 * q + 4, :].bitcast(I32)
+            )
+        for u in range(3, 6):
             load_page(u)
 
         def first_product(u):
@@ -245,7 +245,6 @@ def tile_list_channel_resistance_features_kernel(
         nc.vector.tensor_copy(v[0][:], tab[0][:].indirect(list1[:]))
         quantize(w1_codes[1][0][:], w1_scale[1][0][:], w1_bf[1][0][:])
         nc.vector.tensor_copy(v[1][:], tab[1][:].indirect(list1[:]))
-        deal(w2_sc[0][:], w2_sc_raw[:])
         deal(w2_dealt[:].bitcast(U16), w2_raw[:].bitcast(U16))
         for u in range(PACK):
             first_product(u)
@@ -257,14 +256,18 @@ def tile_list_channel_resistance_features_kernel(
             if u in (1, 2):
                 cast_w1(nc.scalar.copy, u - 1, 1)
                 quantize(w1_codes[u - 1][1][:], w1_scale[u - 1][1][:], w1_bf[u - 1][1][:])
+        deal(w2_sc[0][:], w2_sc_raw[:])
         for q in range(4):
-            nc.gpsimd.dma_start(
+            nc.sync.dma_start(
                 out=w2_sc[1][32 * q : 32 * q + 4, :].bitcast(I32), in_=w2_sc[0][32 * q + 4 : 32 * q + 8, :].bitcast(I32)
             )
         for u in range(PACK, 2 * PACK):
             first_product(u)
         place(4)
         combine(3)
+        for u in (6, 7):
+            pages.append(tile("page%d" % u, [P, T2], F32, tag="then_page%d" % u))
+            load_page(u)
         place(5)
         second_product(0, 0, M)
         place(6)

@@ -1,6 +1,7 @@
 from contextlib import ExitStack
 
 import concourse.mybir as mybir
+from concourse.masks import make_identity
 
 K, T, S, H, T2, M, N = 1024, 2048, 512, 1024, 1024, 512, 1024
 FLOPS = 2 * K * H * S + 2 * H * N * M
@@ -53,16 +54,19 @@ def tile_list_channel_resistance_features_kernel(
         v = [tile("v%d" % a, [P, S], U32) for a in range(2)]
         v_sc = tile("v_sc", [P, S], U8)
         w2_raw = tile("w2_raw", [P, 4 * N], U8)
-        w2_dealt = tile("w2_dealt", [P, 4 * N], U8)
         w2_sc_raw = tile("w2_sc_raw", [P, N], U8)
         w2_sc = [tile("w2_sc%d" % b, [P, N], U8) for b in range(2)]
         gain_t = tile("gain_t", [P, 8], F32)
         freq_t = tile("freq_t", [P, 8], F32)
         amp_t = tile("amp_t", [P, 8], F32)
         wgs_first = tile("wgs_first", [P, S], F32, tag="then_page6")
-        wgs_rest = tile("wgs_rest", [P, 3 * S], F32)
+        wgs_t = [wgs_first] + [tile("wgs%d" % i, [P, S], F32) for i in range(1, PACK)]
         wgt_t = tile("wgt_t", [P, M], F32)
-        x_wide = tile("x_wide", [P, 2 * M], F32, tag="then_page7")
+        x_wide = tile("x_wide", [P, 2 * M], F32)
+        wgs_raw = tile("wgs_raw", [P, S], F32)
+        wgs_turned = [tile("wgs_turned%d" % i, [P, S], F32) for i in range(PACK)]
+        ident = tile("ident", [P, P], F32)
+        w2_dealt = tile("w2_dealt", [P, 4 * N], U8)
         pages = [tile("page%d" % u, [P, T2], F32) for u in range(6)]
         h = tile("h", [P, 8 * S], F32)
         ripple = tile("ripple", [P, 2 * M], F32)
@@ -85,26 +89,38 @@ def tile_list_channel_resistance_features_kernel(
                 out=dst[:].rearrange("p (b i) -> p b i", b=2), in_=src.rearrange("(b p i) -> p b i", b=2, i=PACK)
             )
 
+        def deal_wgs(i):
+            turned = banks[3][:].rearrange("j (c q i) -> j i c q", c=4, i=PACK)[:, i]
+            nc.scalar.copy(
+                out=wgs_turned[i][:].rearrange("j (c r q) -> j c r q", c=4, r=4),
+                in_=turned.unsqueeze(2).to_broadcast([P, 4, 4, 32]),
+            )
+            for c in range(4):
+                cols = slice(c * P, (c + 1) * P)
+                nc.tensor.transpose(banks[4 + i][:, cols], wgs_turned[i][:, cols], ident[:])
+            nc.scalar.copy(out=wgs_t[i][:], in_=banks[4 + i][:])
+
         def cast_w1(copy, a, b):
             copy(
-                out=w1_bf[a][b][:].rearrange("p (i m j) -> p m j i", i=PACK, j=PACK),
-                in_=w1_raw[a][b][:].rearrange("p j (m i) -> p m j i", i=PACK),
+                out=w1_bf[a][b][:].rearrange("p (i m j) -> p m i j", i=PACK, j=PACK),
+                in_=w1_raw[a][b][:].rearrange("p j (m i) -> p m i j", i=PACK),
             )
 
         def quantize(codes, scale, values):
             nc.vector.quantize_mx(out=codes.bitcast(FP8X4), scales=scale, in_=values)
 
-        nc.gpsimd.memset(tab_sc[:].bitcast(I32), 0)
+        make_identity(nc, ident[:])
+        nc.vector.memset(tab_sc[:].bitcast(I32), 0)
         nc.vector.memset(w2_sc_raw[:].bitcast(I32), 0)
         nc.vector.memset(w2_sc[1][:].bitcast(I32), 0)
-        nc.sync.dma_start(list1[:], offs)
-        nc.sync.dma_start(list2[:], offs2)
-        load_rows(gain_t, gain)
-        load_w1(0, 0)
         for q in range(4):
-            nc.scalar.dma_start(
+            nc.gpsimd.dma_start(
                 out=tab_sc[32 * q : 32 * q + 8, :].bitcast(I32), in_=tab_scales[:, 4 * q : 4 * q + 4, :].bitcast(I32)
             )
+        nc.sync.dma_start(out=wgs_raw[:], in_=wgs)
+        load_w1(0, 0)
+        nc.sync.dma_start(list1[:], offs)
+        nc.sync.dma_start(list2[:], offs2)
         load_w1(1, 0)
         load_tab(0)
         load_tab(1)
@@ -112,14 +128,8 @@ def tile_list_channel_resistance_features_kernel(
             out=w2_raw[:].bitcast(I32).rearrange("p (b c) -> p b c", b=2),
             in_=w2_words.bitcast(I32).rearrange("b p c -> p b c"),
         )
+        load_rows(gain_t, gain)
         load_page(0)
-        wgs_rows = wgs.rearrange("(q i) j -> q i j", i=PACK)
-        for q in range(4):
-            nc.sync.dma_start(out=wgs_first[32 * q : 32 * q + 32, :], in_=wgs_rows[:, 0, :])
-        for q in range(4):
-            nc.sync.dma_start(
-                out=wgs_rest[32 * q : 32 * q + 32, :], in_=wgs_rows[:, 1:PACK, :].rearrange("q i j -> q (i j)")
-            )
         nc.sync.dma_start(out=wgt_t[:], in_=wgt)
         nc.sync.dma_start(list3[:], offs3)
         load_rows(freq_t, freq)
@@ -128,12 +138,13 @@ def tile_list_channel_resistance_features_kernel(
         load_w1(0, 1)
         load_page(2)
         load_w1(1, 1)
+        load_page(3)
         for q in range(4):
             nc.sync.dma_start(
                 out=w2_sc_raw[32 * q : 32 * q + 8, :].bitcast(I32), in_=w2_scales[:, 4 * q : 4 * q + 4, :].bitcast(I32)
             )
-        for u in range(3, 6):
-            load_page(u)
+        load_page(4)
+        load_page(5)
 
         def first_product(u):
             b, i = divmod(u, PACK)
@@ -152,7 +163,7 @@ def tile_list_channel_resistance_features_kernel(
 
         def place(u):
             i = u % PACK
-            weights = wgs_first[:] if i == 0 else wgs_rest[:, (i - 1) * S : i * S]
+            weights = wgs_t[i][:]
             nc.vector.tensor_tensor(pages[u][:].indirect(list2[:]), h[:, u * S : (u + 1) * S], weights, MULT)
 
         def deal(dst, src):
@@ -178,12 +189,14 @@ def tile_list_channel_resistance_features_kernel(
         steps = [(u, 0, M) for u in range(PACK)]
         steps += [(u, c * W, W) for c in range(CHUNKS) for u in range(PACK, 2 * PACK)]
 
+        x_tiles = [x_wide[:, (k % 2) * M : (k % 2 + 1) * M] for k in range(3)]
+
         def buffers(k):
             u, m0, w = steps[k]
             if w == M:
-                return x_wide[:, (k % 2) * M : (k % 2 + 1) * M], ripple[:, (k % 2) * M : (k % 2 + 1) * M]
+                return x_tiles[k], ripple[:, (k % 2) * M : (k % 2 + 1) * M]
             slot = k % RING
-            return wgs_rest[:, 2 * S + slot * W : 2 * S + (slot + 1) * W], ripple[:, slot * W : (slot + 1) * W]
+            return wgs_t[3][:, slot * W : (slot + 1) * W], ripple[:, slot * W : (slot + 1) * W]
 
         def pick(k):
             u, m0, w = steps[k]
@@ -238,6 +251,10 @@ def tile_list_channel_resistance_features_kernel(
                 in_=y_codes[:].bitcast(I32).rearrange("p (g m) -> p g m", g=2)[:, :, c * W : (c + 1) * W],
             )
 
+        for c in range(4):
+            cols = slice(c * P, (c + 1) * P)
+            nc.tensor.transpose(banks[3][:, cols], wgs_raw[:, cols], ident[:])
+        deal_wgs(0)
         cast_w1(nc.vector.tensor_copy, 0, 0)
         nc.vector.tensor_copy(v_sc[:], tab_sc[:].indirect(list1[:]))
         quantize(w1_codes[0][0][:], w1_scale[0][0][:], w1_bf[0][0][:])
@@ -246,16 +263,22 @@ def tile_list_channel_resistance_features_kernel(
         quantize(w1_codes[1][0][:], w1_scale[1][0][:], w1_bf[1][0][:])
         nc.vector.tensor_copy(v[1][:], tab[1][:].indirect(list1[:]))
         deal(w2_dealt[:].bitcast(U16), w2_raw[:].bitcast(U16))
-        for u in range(PACK):
+        first_product(0)
+        for u in range(1, PACK):
+            deal_wgs(u)
+        for u in range(1, PACK):
             first_product(u)
         for u in range(PACK):
             place(u)
             if u > 0:
                 combine(u - 1)
+            if u in (2, 3):
+                quantize(w1_codes[u - 2][1][:], w1_scale[u - 2][1][:], w1_bf[u - 2][1][:])
+            if u == 3:
+                x_tiles.append(tile("x_last", [P, M], F32, tag="w1_bf11")[:])
             pick(u)
             if u in (1, 2):
                 cast_w1(nc.scalar.copy, u - 1, 1)
-                quantize(w1_codes[u - 1][1][:], w1_scale[u - 1][1][:], w1_bf[u - 1][1][:])
         deal(w2_sc[0][:], w2_sc_raw[:])
         for q in range(4):
             nc.sync.dma_start(
@@ -266,7 +289,7 @@ def tile_list_channel_resistance_features_kernel(
         place(4)
         combine(3)
         for u in (6, 7):
-            pages.append(tile("page%d" % u, [P, T2], F32, tag="then_page%d" % u))
+            pages.append(tile("page%d" % u, [P, T2], F32, tag="then_page6" if u == 6 else "w1_bf11"))
             load_page(u)
         place(5)
         second_product(0, 0, M)

@@ -23,8 +23,7 @@ P = 128
 PACK = 4
 PASS = P * PACK
 BANK = 512
-W = 128
-CHUNKS = M // W
+CHUNKS = (256, 128, 128)
 RING = 4
 
 
@@ -47,29 +46,35 @@ def tile_list_channel_resistance_features_kernel(
 
         w1_raw = [[tile("w1_raw%d%d" % (a, b), [P, PACK, PASS], F32) for b in range(2)] for a in range(2)]
         w1_bf = [[tile("w1_bf%d%d" % (a, b), [P, PACK * PASS], BF16) for b in range(2)] for a in range(2)]
-        w1_codes = [[tile("w1_codes%d%d" % (a, b), [P, PASS], U32) for b in range(2)] for a in range(2)]
+        w1_codes = {(a, 0): tile("w1_codes%d0" % a, [P, PASS], U32)[:] for a in range(2)}
         w1_scale = [[tile("w1_scale%d%d" % (a, b), [P, PASS], U8) for b in range(2)] for a in range(2)]
         tab = [tile("tab%d" % a, [P, T], U32) for a in range(2)]
         tab_sc = tile("tab_sc", [P, T], U8)
         v = [tile("v%d" % a, [P, S], U32) for a in range(2)]
         v_sc = tile("v_sc", [P, S], U8)
         w2_raw = tile("w2_raw", [P, 4 * N], U8)
+        w2_dealt = tile("w2_dealt", [P, 4 * N], U8)
         w2_sc_raw = tile("w2_sc_raw", [P, N], U8)
-        w2_sc = [tile("w2_sc%d" % b, [P, N], U8) for b in range(2)]
+        w2_sc = {1: tile("w2_sc1", [P, N], U8)}
         gain_t = tile("gain_t", [P, 8], F32)
         freq_t = tile("freq_t", [P, 8], F32)
         amp_t = tile("amp_t", [P, 8], F32)
-        wgs_first = tile("wgs_first", [P, S], F32, tag="then_page6")
-        wgs_t = [wgs_first] + [tile("wgs%d" % i, [P, S], F32) for i in range(1, PACK)]
-        wgt_t = tile("wgt_t", [P, M], F32)
-        x_wide = tile("x_wide", [P, 2 * M], F32)
-        wgs_raw = tile("wgs_raw", [P, S], F32)
-        wgs_turned = [tile("wgs_turned%d" % i, [P, S], F32) for i in range(PACK)]
         ident = tile("ident", [P, P], F32)
-        w2_dealt = tile("w2_dealt", [P, 4 * N], U8)
-        pages = [tile("page%d" % u, [P, T2], F32) for u in range(6)]
-        h = tile("h", [P, 8 * S], F32)
+        wgs_raw = tile("wgs_raw", [P, S], F32)
+        wgs_turned = [tile("wgs_turned0", [P, S], F32)[:]]
+        wgs_t = [tile("wgs%d" % i, [P, S], F32)[:] for i in range(PACK - 1)]
+        wgt_t = tile("wgt_t", [P, M], F32)
+        pages = [tile("page%d" % u, [P, T2], F32) for u in range(7)]
+        h = [tile("h%d" % u, [P, S], F32) for u in range(8)]
+        x_wide = [tile("x_wide%d" % n, [P, M], F32) for n in range(2)]
         ripple = tile("ripple", [P, 2 * M], F32)
+        z_turned = [tile("z_turned%d" % c, [P, PASS], BF16) for c in range(4)]
+        z_rows = tile("z_rows", [P, PACK * M], BF16)
+        z_bf = [tile("z_bf%d" % b, [P, PACK * M], BF16) for b in range(2)]
+        z_codes = [tile("z_codes%d" % b, [P, M], U32) for b in range(2)]
+        z_scale = [tile("z_scale%d" % b, [P, M], U8) for b in range(2)]
+        y = [[tile("y%d%d" % (c, g), [P, PACK * w], F32) for g in range(2)] for c, w in enumerate(CHUNKS)]
+        y_bf = [[tile("y_bf%d%d" % (c, g), [P, PACK * w], BF16) for g in range(2)] for c, w in enumerate(CHUNKS)]
         y_codes = tile("y_codes", [P, 2 * M], U32)
         y_scale = tile("y_scale", [P, 2 * M], U8)
 
@@ -89,34 +94,17 @@ def tile_list_channel_resistance_features_kernel(
                 out=dst[:].rearrange("p (b i) -> p b i", b=2), in_=src.rearrange("(b p i) -> p b i", b=2, i=PACK)
             )
 
-        def deal_wgs(i):
-            turned = banks[3][:].rearrange("j (c q i) -> j i c q", c=4, i=PACK)[:, i]
-            nc.scalar.copy(
-                out=wgs_turned[i][:].rearrange("j (c r q) -> j c r q", c=4, r=4),
-                in_=turned.unsqueeze(2).to_broadcast([P, 4, 4, 32]),
-            )
-            for c in range(4):
-                cols = slice(c * P, (c + 1) * P)
-                nc.tensor.transpose(banks[4 + i][:, cols], wgs_turned[i][:, cols], ident[:])
-            nc.scalar.copy(out=wgs_t[i][:], in_=banks[4 + i][:])
+        def load_scale_rows(queue, dst, src):
+            for q in range(4):
+                queue.dma_start(
+                    out=dst[32 * q : 32 * q + 8, :].bitcast(I32), in_=src[:, 4 * q : 4 * q + 4, :].bitcast(I32)
+                )
 
-        def cast_w1(copy, a, b):
-            copy(
-                out=w1_bf[a][b][:].rearrange("p (i m j) -> p m i j", i=PACK, j=PACK),
-                in_=w1_raw[a][b][:].rearrange("p j (m i) -> p m i j", i=PACK),
-            )
-
-        def quantize(codes, scale, values):
-            nc.vector.quantize_mx(out=codes.bitcast(FP8X4), scales=scale, in_=values)
-
+        nc.gpsimd.memset(tab_sc[:].bitcast(I32), 0)
+        load_scale_rows(nc.gpsimd, tab_sc, tab_scales)
         make_identity(nc, ident[:])
-        nc.vector.memset(tab_sc[:].bitcast(I32), 0)
         nc.vector.memset(w2_sc_raw[:].bitcast(I32), 0)
         nc.vector.memset(w2_sc[1][:].bitcast(I32), 0)
-        for q in range(4):
-            nc.gpsimd.dma_start(
-                out=tab_sc[32 * q : 32 * q + 8, :].bitcast(I32), in_=tab_scales[:, 4 * q : 4 * q + 4, :].bitcast(I32)
-            )
         nc.sync.dma_start(out=wgs_raw[:], in_=wgs)
         load_w1(0, 0)
         nc.sync.dma_start(list1[:], offs)
@@ -136,35 +124,36 @@ def tile_list_channel_resistance_features_kernel(
         load_page(1)
         load_rows(amp_t, amp)
         load_w1(0, 1)
-        load_page(2)
         load_w1(1, 1)
-        load_page(3)
-        for q in range(4):
-            nc.sync.dma_start(
-                out=w2_sc_raw[32 * q : 32 * q + 8, :].bitcast(I32), in_=w2_scales[:, 4 * q : 4 * q + 4, :].bitcast(I32)
+        load_page(2)
+        load_scale_rows(nc.sync, w2_sc_raw, w2_scales)
+        for u in range(3, 7):
+            load_page(u)
+
+        def repeat_wgs(i):
+            turned = banks[3][:].rearrange("j (c q i) -> j i c q", c=4, i=PACK)[:, i]
+            nc.scalar.copy(
+                out=wgs_turned[i].rearrange("j (c r q) -> j c r q", c=4, r=4),
+                in_=turned.unsqueeze(2).to_broadcast([P, 4, 4, 32]),
             )
-        load_page(4)
-        load_page(5)
 
-        def first_product(u):
-            b, i = divmod(u, PACK)
-            cols = slice(i * P, (i + 1) * P)
-            for a in range(2):
-                nc.tensor.matmul_mx(
-                    out=banks[u][:],
-                    lhsT=w1_codes[a][b][:, cols].bitcast(FP8X4),
-                    lhsT_scale=w1_scale[a][b][:, cols],
-                    rhs=v[a][:].bitcast(FP8X4),
-                    rhs_scale=v_sc[4 * a : P, :],
-                    start=(a == 0),
-                    stop=(a == 1),
-                )
-            nc.scalar.activation(out=h[:, u * S : (u + 1) * S], in_=banks[u][:], func=COPY, scale=gain_t[:, u : u + 1])
+        def turn_wgs(i, bank):
+            for c in range(4):
+                cols = slice(c * P, (c + 1) * P)
+                nc.tensor.transpose(bank[:, cols], wgs_turned[i][:, cols], ident[:])
+            nc.scalar.copy(out=wgs_t[i], in_=bank[:])
 
-        def place(u):
-            i = u % PACK
-            weights = wgs_t[i][:]
-            nc.vector.tensor_tensor(pages[u][:].indirect(list2[:]), h[:, u * S : (u + 1) * S], weights, MULT)
+        def cast_w1(copy, a, b):
+            copy(
+                out=w1_bf[a][b][:].rearrange("p (i m j) -> p m i j", i=PACK, j=PACK),
+                in_=w1_raw[a][b][:].rearrange("p j (m i) -> p m i j", i=PACK),
+            )
+
+        def quantize(codes, scale, values):
+            nc.vector.quantize_mx(out=codes.bitcast(FP8X4), scales=scale, in_=values)
+
+        def quantize_w1(a, b):
+            quantize(w1_codes[a, b], w1_scale[a][b][:], w1_bf[a][b][:])
 
         def deal(dst, src):
             nc.vector.tensor_copy(
@@ -172,13 +161,51 @@ def tile_list_channel_resistance_features_kernel(
                 in_=src.rearrange("p (a mb mi t) -> p a mb t mi", t=PACK, mb=16, mi=8),
             )
 
-        z_rows = [h[:, S : 5 * S], tile("z_rows", [P, PACK * M], BF16)[:]]
-        z_bf = [tile("z_bf%d" % b, [P, PACK * M], BF16) for b in range(2)]
-        z_codes = [tile("z_codes%d" % b, [P, M], U32) for b in range(2)]
-        z_scale = [tile("z_scale%d" % b, [P, M], U8) for b in range(2)]
-        y = [[tile("y%d%d" % (c, g), [P, BANK], F32) for g in range(2)] for c in range(CHUNKS)]
-        y_bf = [[tile("y_bf%d%d" % (c, g), [P, BANK], BF16) for g in range(2)] for c in range(CHUNKS)]
-        last = CHUNKS - 1
+        def first_product(u):
+            b, i = divmod(u, PACK)
+            cols = slice(i * P, (i + 1) * P)
+            for a in range(2):
+                nc.tensor.matmul_mx(
+                    out=banks[i][:],
+                    lhsT=w1_codes[a, b][:, cols].bitcast(FP8X4),
+                    lhsT_scale=w1_scale[a][b][:, cols],
+                    rhs=v[a][:].bitcast(FP8X4),
+                    rhs_scale=v_sc[4 * a : P, :],
+                    start=(a == 0),
+                    stop=(a == 1),
+                )
+            nc.scalar.activation(out=h[u][:], in_=banks[i][:], func=COPY, scale=gain_t[:, u : u + 1])
+
+        def place(u):
+            nc.vector.tensor_tensor(pages[u][:].indirect(list2[:]), h[u][:], wgs_t[u % PACK], MULT)
+
+        def pick(u, m0, w, x, s):
+            offsets = list3[:, m0 // 16 : (m0 + w) // 16]
+            nc.vector.tensor_tensor(x, pages[u][:].indirect(offsets), wgt_t[:, m0 : m0 + w], MULT)
+            nc.scalar.activation(out=s, in_=x, func=SIN, scale=freq_t[:, u : u + 1])
+
+        def add_turned(u, x, s):
+            nc.scalar.activation(out=s, in_=s, func=COPY, scale=amp_t[:, u : u + 1])
+            for c in range(4):
+                cols = slice(c * P, (c + 1) * P)
+                for term, first in ((x, True), (s, False)):
+                    nc.tensor.matmul(
+                        banks[4 + c][:, u * P : (u + 1) * P], term[:, cols], ident[:],
+                        start=first, stop=not first, is_transpose=True,
+                    )
+
+        def turn_back(c):
+            nc.scalar.copy(
+                out=z_turned[c][:].rearrange("m (p i) -> m p i", i=PACK),
+                in_=banks[4 + c][:].rearrange("m (i p) -> m p i", i=PACK),
+            )
+            pairs = z_turned[c][:].bitcast(F32)
+            for e in range(2):
+                nc.tensor.transpose(banks[4 + c][:, e * P : (e + 1) * P], pairs[:, e : 2 * P : 2], ident[:])
+            nc.scalar.copy(
+                out=z_bf[0][:, c * PASS : (c + 1) * PASS].bitcast(F32).rearrange("p (m e) -> p m e", e=2),
+                in_=banks[4 + c][:, 0 : 2 * P].rearrange("p (e m) -> p m e", e=2),
+            )
 
         def interleave(copy, dst, src):
             copy(
@@ -186,129 +213,142 @@ def tile_list_channel_resistance_features_kernel(
                 in_=src.rearrange("p (t c i) -> p c t i", i=4, t=PACK),
             )
 
-        steps = [(u, 0, M) for u in range(PACK)]
-        steps += [(u, c * W, W) for c in range(CHUNKS) for u in range(PACK, 2 * PACK)]
+        starts = [sum(CHUNKS[:c]) for c in range(len(CHUNKS))]
+        chunk_banks = [banks[m0 // 64 : (m0 + w) // 64] for m0, w in zip(starts, CHUNKS)]
+        last = len(CHUNKS) - 1
 
-        x_tiles = [x_wide[:, (k % 2) * M : (k % 2 + 1) * M] for k in range(3)]
-
-        def buffers(k):
-            u, m0, w = steps[k]
-            if w == M:
-                return x_tiles[k], ripple[:, (k % 2) * M : (k % 2 + 1) * M]
-            slot = k % RING
-            return wgs_t[3][:, slot * W : (slot + 1) * W], ripple[:, slot * W : (slot + 1) * W]
-
-        def pick(k):
-            u, m0, w = steps[k]
-            x, s = buffers(k)
-            offsets = list3[:, m0 // 16 : (m0 + w) // 16]
-            nc.vector.tensor_tensor(x, pages[u][:].indirect(offsets), wgt_t[:, m0 : m0 + w], MULT)
-            nc.scalar.activation(out=s, in_=x, func=SIN, scale=freq_t[:, u : u + 1])
-
-        def combine(k):
-            u, m0, w = steps[k]
-            b, i = divmod(u, PACK)
-            x, s = buffers(k)
-            rows = z_rows[b][:, PACK * m0 : PACK * (m0 + w)]
-            nc.vector.scalar_tensor_tensor(
-                out=rows[:, i * w : (i + 1) * w], in0=s, scalar=amp_t[:, u : u + 1], in1=x, op0=MULT, op1=ADD
-            )
-            if i == PACK - 1:
-                copy = nc.vector.tensor_copy if k == len(steps) - 1 else nc.scalar.copy
-                interleave(copy, z_bf[b][:, PACK * m0 : PACK * (m0 + w)], rows)
-
-        def second_product(b, m0, w):
-            quantize(z_codes[b][:, m0 : m0 + w], z_scale[b][:, m0 : m0 + w], z_bf[b][:, PACK * m0 : PACK * (m0 + w)])
-            for c in range(m0 // W, (m0 + w) // W):
-                for n in range(8):
-                    g, t = divmod(n, PACK)
-                    at = b * N + n * P
-                    nc.tensor.matmul_mx(
-                        out=banks[2 * c + g][:, t * W : (t + 1) * W],
-                        lhsT=w2_dealt[:, 2 * at : 2 * (at + P)].bitcast(FP4X4),
-                        lhsT_scale=w2_sc[b][:, n * P : (n + 1) * P],
-                        rhs=z_codes[b][:, c * W : (c + 1) * W].bitcast(FP8X4),
-                        rhs_scale=z_scale[b][:, c * W : (c + 1) * W],
-                        start=(b == 0 and t == 0),
-                        stop=(b == 1 and t == PACK - 1),
-                    )
+        def second_product(b, c):
+            m0, w = starts[c], CHUNKS[c]
+            per_bank = BANK // w
+            for n in range(8):
+                slot = n % per_bank
+                nc.tensor.matmul_mx(
+                    out=chunk_banks[c][n // per_bank][:, slot * w : (slot + 1) * w],
+                    lhsT=w2_dealt[:, 2 * (b * N + n * P) : 2 * (b * N + (n + 1) * P)].bitcast(FP4X4),
+                    lhsT_scale=w2_sc[b][:, n * P : (n + 1) * P],
+                    rhs=z_codes[b][:, m0 : m0 + w].bitcast(FP8X4),
+                    rhs_scale=z_scale[b][:, m0 : m0 + w],
+                    start=(b == 0 and slot == 0),
+                    stop=(b == 1 and slot == per_bank - 1),
+                )
 
         def take_out(c, g):
-            on_vector = c == last and g == 1
-            (nc.vector.tensor_copy if on_vector else nc.scalar.copy)(out=y[c][g][:], in_=banks[2 * c + g][:])
+            m0, w = starts[c], CHUNKS[c]
+            per_group = len(chunk_banks[c]) // 2
+            copy = nc.vector.tensor_copy if (c == last and g == 1) else nc.scalar.copy
+            for n in range(per_group):
+                copy(out=y[c][g][:, n * BANK : (n + 1) * BANK], in_=chunk_banks[c][g * per_group + n][:])
             nc.sync.dma_start(
-                out=out_0.rearrange("(g p t) m -> g p t m", g=2, t=PACK)[g, :, :, c * W : (c + 1) * W],
+                out=out_0.rearrange("(g p t) m -> g p t m", g=2, t=PACK)[g, :, :, m0 : m0 + w],
                 in_=y[c][g][:].rearrange("p (t m) -> p t m", t=PACK),
             )
-            interleave(nc.vector.tensor_copy if g == 1 else nc.scalar.copy, y_bf[c][g][:], y[c][g][:])
+            interleave(nc.vector.tensor_copy if (g == 1 or c == 0) else nc.scalar.copy, y_bf[c][g][:], y[c][g][:])
 
         def planes(c):
+            m0, w = starts[c], CHUNKS[c]
             for g in range(2):
-                cols = slice(g * M + c * W, g * M + (c + 1) * W)
+                cols = slice(g * M + m0, g * M + m0 + w)
                 quantize(y_codes[:, cols], y_scale[:, cols], y_bf[c][g][:])
             nc.sync.dma_start(
-                out=out_1.rearrange("g p m t -> p g (m t)").bitcast(I32)[:, :, c * W : (c + 1) * W],
-                in_=y_codes[:].bitcast(I32).rearrange("p (g m) -> p g m", g=2)[:, :, c * W : (c + 1) * W],
+                out=out_1.rearrange("g p m t -> p g (m t)").bitcast(I32)[:, :, m0 : m0 + w],
+                in_=y_codes[:].bitcast(I32).rearrange("p (g m) -> p g m", g=2)[:, :, m0 : m0 + w],
             )
 
         for c in range(4):
             cols = slice(c * P, (c + 1) * P)
             nc.tensor.transpose(banks[3][:, cols], wgs_raw[:, cols], ident[:])
-        deal_wgs(0)
+        repeat_wgs(0)
+        turn_wgs(0, banks[4])
         cast_w1(nc.vector.tensor_copy, 0, 0)
         nc.vector.tensor_copy(v_sc[:], tab_sc[:].indirect(list1[:]))
-        quantize(w1_codes[0][0][:], w1_scale[0][0][:], w1_bf[0][0][:])
+        quantize_w1(0, 0)
         cast_w1(nc.scalar.copy, 1, 0)
         nc.vector.tensor_copy(v[0][:], tab[0][:].indirect(list1[:]))
-        quantize(w1_codes[1][0][:], w1_scale[1][0][:], w1_bf[1][0][:])
+        quantize_w1(1, 0)
         nc.vector.tensor_copy(v[1][:], tab[1][:].indirect(list1[:]))
         deal(w2_dealt[:].bitcast(U16), w2_raw[:].bitcast(U16))
         first_product(0)
-        for u in range(1, PACK):
-            deal_wgs(u)
+        turned_rest = tile("turned_rest", [P, 3 * S], F32, tag="w1_raw10")
+        for i in range(1, PACK):
+            wgs_turned.append(turned_rest[:, (i - 1) * S : i * S])
+            repeat_wgs(i)
         for u in range(1, PACK):
             first_product(u)
+            if u < PACK - 1:
+                turn_wgs(u, banks[u - 1])
+
         for u in range(PACK):
+            if u == 1:
+                cast_w1(nc.scalar.copy, 0, 1)
+                cast_w1(nc.scalar.copy, 1, 1)
+                after_cast = tile("after_cast", [P, M + S], F32, tag="w1_raw11")
+                wgs_t.append(after_cast[:, M : M + S])
+                turn_wgs(PACK - 1, banks[2])
             place(u)
-            if u > 0:
-                combine(u - 1)
-            if u in (2, 3):
-                quantize(w1_codes[u - 2][1][:], w1_scale[u - 2][1][:], w1_bf[u - 2][1][:])
-            if u == 3:
-                x_tiles.append(tile("x_last", [P, M], F32, tag="w1_bf11")[:])
-            pick(u)
-            if u in (1, 2):
-                cast_w1(nc.scalar.copy, u - 1, 1)
+            x = x_wide[u % 2][:]
+            s = after_cast[:, 0:M] if u % 2 else ripple[:, 0:M]
+            pick(u, 0, M, x, s)
+            add_turned(u, x, s)
+            if u == 2:
+                late_codes = tile("late_codes", [P, 2 * PASS], U32, tag="h2")
+                for a in range(2):
+                    w1_codes[a, 1] = late_codes[:, a * PASS : (a + 1) * PASS]
+                    quantize_w1(a, 1)
+                for later in range(PACK, 2 * PACK):
+                    first_product(later)
+        w2_sc[0] = tile("w2_sc0", [P, N], U8, tag="h3")
         deal(w2_sc[0][:], w2_sc_raw[:])
         for q in range(4):
             nc.sync.dma_start(
                 out=w2_sc[1][32 * q : 32 * q + 4, :].bitcast(I32), in_=w2_sc[0][32 * q + 4 : 32 * q + 8, :].bitcast(I32)
             )
-        for u in range(PACK, 2 * PACK):
-            first_product(u)
-        place(4)
-        combine(3)
-        for u in (6, 7):
-            pages.append(tile("page%d" % u, [P, T2], F32, tag="then_page6" if u == 6 else "w1_bf11"))
-            load_page(u)
-        place(5)
-        second_product(0, 0, M)
-        place(6)
+        for c in range(4):
+            turn_back(c)
+        pages.append(tile("page7", [P, T2], F32, tag="z_turned0"))
+        load_page(7)
+        for u in range(PACK, 7):
+            place(u)
+        quantize(z_codes[0][:], z_scale[0][:], z_bf[0][:])
+        for c in range(len(CHUNKS)):
+            second_product(0, c)
         place(7)
-        for k in range(PACK, len(steps) + 8):
+
+        steps = [(c, u) for c in range(len(CHUNKS)) for u in range(PACK, 2 * PACK)]
+        x_ring = [h[7][:, 0:256], h[7][:, 256:512], wgs_t[3][:, 0:256], wgs_t[3][:, 256:512]]
+
+        def buffers(k):
+            w = CHUNKS[steps[k][0]]
+            slot = k % RING
+            return x_ring[slot][:, 0:w], ripple[:, slot * 256 : slot * 256 + w]
+
+        def combine(k):
+            c, u = steps[k]
+            m0, w = starts[c], CHUNKS[c]
+            i = u - PACK
+            x, s = buffers(k)
+            rows = z_rows[:, PACK * m0 : PACK * (m0 + w)]
+            nc.vector.scalar_tensor_tensor(
+                out=rows[:, i * w : (i + 1) * w], in0=s, scalar=amp_t[:, u : u + 1], in1=x, op0=MULT, op1=ADD
+            )
+            if i == PACK - 1:
+                copy = nc.vector.tensor_copy if c == last else nc.scalar.copy
+                interleave(copy, z_bf[1][:, PACK * m0 : PACK * (m0 + w)], rows)
+
+        for k in range(len(steps) + 8):
             if k < len(steps):
-                pick(k)
-            if PACK <= k - 1 < len(steps):
+                c, u = steps[k]
+                pick(u, starts[c], CHUNKS[c], *buffers(k))
+            if 0 <= k - 1 < len(steps):
                 combine(k - 1)
-            j = k - 3
-            if PACK <= j < len(steps) and j % PACK == PACK - 1:
-                u, m0, w = steps[j]
-                second_product(1, m0, w)
-                take_out(m0 // W, 0)
-                take_out(m0 // W, 1)
-            j = k - 6
-            if PACK <= j < len(steps) and j % PACK == PACK - 1:
-                planes(steps[j][1] // W)
+            if 0 <= k - 3 < len(steps) and (k - 3) % PACK == PACK - 1:
+                c = steps[k - 3][0]
+                m0, w = starts[c], CHUNKS[c]
+                quantize(z_codes[1][:, m0 : m0 + w], z_scale[1][:, m0 : m0 + w], z_bf[1][:, PACK * m0 : PACK * (m0 + w)])
+                second_product(1, c)
+                take_out(c, 0)
+                take_out(c, 1)
+            if 0 <= k - 6 < len(steps) and (k - 6) % PACK == PACK - 1:
+                planes(steps[k - 6][0])
 
         for q in range(4):
             queue = nc.sync if q % 2 == 0 else nc.scalar

@@ -25,6 +25,7 @@ PASS = P * PACK
 BANK = 512
 CHUNKS = (256, 128, 128)
 RING = 4
+CAST_SPLIT = 88
 
 
 def tile_list_channel_resistance_features_kernel(
@@ -50,10 +51,7 @@ def tile_list_channel_resistance_features_kernel(
         w1_scale = [[tile("w1_scale%d%d" % (a, b), [P, PASS], U8) for b in range(2)] for a in range(2)]
         tab = [tile("tab%d" % a, [P, T], U32) for a in range(2)]
         tab_sc = tile("tab_sc", [P, T], U8)
-        v = [tile("v%d" % a, [P, S], U32) for a in range(2)]
-        v_sc = tile("v_sc", [P, S], U8)
         w2_raw = tile("w2_raw", [P, 4 * N], U8)
-        w2_dealt = tile("w2_dealt", [P, 4 * N], U8)
         w2_sc_raw = tile("w2_sc_raw", [P, N], U8)
         w2_sc = {1: tile("w2_sc1", [P, N], U8)}
         gain_t = tile("gain_t", [P, 8], F32)
@@ -100,9 +98,9 @@ def tile_list_channel_resistance_features_kernel(
                     out=dst[32 * q : 32 * q + 8, :].bitcast(I32), in_=src[:, 4 * q : 4 * q + 4, :].bitcast(I32)
                 )
 
-        nc.gpsimd.memset(tab_sc[:].bitcast(I32), 0)
-        load_scale_rows(nc.gpsimd, tab_sc, tab_scales)
         make_identity(nc, ident[:])
+        nc.vector.memset(tab_sc[:].bitcast(I32), 0)
+        load_scale_rows(nc.gpsimd, tab_sc, tab_scales)
         nc.vector.memset(w2_sc_raw[:].bitcast(I32), 0)
         nc.vector.memset(w2_sc[1][:].bitcast(I32), 0)
         nc.sync.dma_start(out=wgs_raw[:], in_=wgs)
@@ -143,10 +141,10 @@ def tile_list_channel_resistance_features_kernel(
                 nc.tensor.transpose(bank[:, cols], wgs_turned[i][:, cols], ident[:])
             nc.scalar.copy(out=wgs_t[i], in_=bank[:])
 
-        def cast_w1(copy, a, b):
+        def cast_w1(copy, a, b, m0, m1):
             copy(
-                out=w1_bf[a][b][:].rearrange("p (i m j) -> p m i j", i=PACK, j=PACK),
-                in_=w1_raw[a][b][:].rearrange("p j (m i) -> p m i j", i=PACK),
+                out=w1_bf[a][b][:].rearrange("p (i m j) -> p m i j", i=PACK, j=PACK)[:, m0:m1],
+                in_=w1_raw[a][b][:].rearrange("p j (m i) -> p m i j", i=PACK)[:, m0:m1],
             )
 
         def quantize(codes, scale, values):
@@ -164,15 +162,16 @@ def tile_list_channel_resistance_features_kernel(
         def first_product(u):
             b, i = divmod(u, PACK)
             cols = slice(i * P, (i + 1) * P)
-            for a in range(2):
+            order = (0, 1) if u == 0 or b == 1 else (1, 0)
+            for a in order:
                 nc.tensor.matmul_mx(
                     out=banks[i][:],
                     lhsT=w1_codes[a, b][:, cols].bitcast(FP8X4),
                     lhsT_scale=w1_scale[a][b][:, cols],
                     rhs=v[a][:].bitcast(FP8X4),
                     rhs_scale=v_sc[4 * a : P, :],
-                    start=(a == 0),
-                    stop=(a == 1),
+                    start=(a == order[0]),
+                    stop=(a == order[1]),
                 )
             nc.scalar.activation(out=h[u][:], in_=banks[i][:], func=COPY, scale=gain_t[:, u : u + 1])
 
@@ -259,13 +258,17 @@ def tile_list_channel_resistance_features_kernel(
             nc.tensor.transpose(banks[3][:, cols], wgs_raw[:, cols], ident[:])
         repeat_wgs(0)
         turn_wgs(0, banks[4])
-        cast_w1(nc.vector.tensor_copy, 0, 0)
-        nc.vector.tensor_copy(v_sc[:], tab_sc[:].indirect(list1[:]))
-        quantize_w1(0, 0)
-        cast_w1(nc.scalar.copy, 1, 0)
+        for a in range(2):
+            cast_w1(nc.vector.tensor_copy, a, 0, 0, CAST_SPLIT)
+            cast_w1(nc.scalar.copy, a, 0, CAST_SPLIT, P)
+            quantize_w1(a, 0)
+        v = [tile("v0", [P, S], U32, tag="w1_bf10")]
         nc.vector.tensor_copy(v[0][:], tab[0][:].indirect(list1[:]))
-        quantize_w1(1, 0)
+        v_sc = tile("v_sc", [P, S], U8, tag="tab0")
+        nc.vector.tensor_copy(v_sc[:], tab_sc[:].indirect(list1[:]))
+        v.append(tile("v1", [P, S], U32, tag="tab_sc"))
         nc.vector.tensor_copy(v[1][:], tab[1][:].indirect(list1[:]))
+        w2_dealt = tile("w2_dealt", [P, 4 * N], U8, tag="tab1")
         deal(w2_dealt[:].bitcast(U16), w2_raw[:].bitcast(U16))
         first_product(0)
         turned_rest = tile("turned_rest", [P, 3 * S], F32, tag="w1_raw10")
@@ -279,8 +282,8 @@ def tile_list_channel_resistance_features_kernel(
 
         for u in range(PACK):
             if u == 1:
-                cast_w1(nc.scalar.copy, 0, 1)
-                cast_w1(nc.scalar.copy, 1, 1)
+                cast_w1(nc.scalar.copy, 0, 1, 0, P)
+                cast_w1(nc.scalar.copy, 1, 1, 0, P)
                 after_cast = tile("after_cast", [P, M + S], F32, tag="w1_raw11")
                 wgs_t.append(after_cast[:, M : M + S])
                 turn_wgs(PACK - 1, banks[2])

from contextlib import ExitStack

import concourse.mybir as mybir
from concourse.masks import make_identity

K, T, S, H, T2, M, N = 1024, 2048, 512, 1024, 1024, 512, 1024
FLOPS = 2 * K * H * S + 2 * H * N * M

F32 = mybir.dt.float32
BF16 = mybir.dt.bfloat16
I32 = mybir.dt.int32
U32 = mybir.dt.uint32
U16 = mybir.dt.uint16
U8 = mybir.dt.uint8
FP8X4 = mybir.dt.float8_e4m3fn_x4
FP4X4 = mybir.dt.float4_e2m1fn_x4
MULT = mybir.AluOpType.mult
ADD = mybir.AluOpType.add
COPY = mybir.ActivationFunctionType.Copy
SIN = mybir.ActivationFunctionType.Sin

P = 128
PACK = 4
PASS = P * PACK
BANK = 512
CHUNKS = (256, 128, 128)
RING = 4
CAST_SPLIT = 88


def tile_list_channel_resistance_features_kernel(
    tc, tab_words, tab_scales, offs, offs2, offs3, w1, gain, page0, wgs, wgt, freq, amp,
    w2_words, w2_scales, out_0, out_1, out_2,
):
    nc = tc.nc
    with ExitStack() as ctx:
        keep = ctx.enter_context(tc.tile_pool(name="keep", bufs=1))
        psum = ctx.enter_context(tc.psum_pool(name="psum", bufs=1))

        def tile(name, shape, dtype, tag=None):
            return keep.tile(shape, dtype, name=name, tag=tag or name, align_bytes=64)

        list1 = keep.tile([P, S // 16], U16, name="list1")
        list2 = keep.tile([P, S // 16], U16, name="list2")
        list3 = keep.tile([P, M // 16], U16, name="list3")
        banks = [psum.tile([P, BANK], F32, name="bank%d" % n) for n in range(8)]

        w1_raw = [[tile("w1_raw%d%d" % (a, b), [P, PACK, PASS], F32) for b in range(2)] for a in range(2)]
        w1_bf = [[tile("w1_bf%d%d" % (a, b), [P, PACK * PASS], BF16) for b in range(2)] for a in range(2)]
        w1_codes = {(a, 0): tile("w1_codes%d0" % a, [P, PASS], U32)[:] for a in range(2)}
        w1_scale = [[tile("w1_scale%d%d" % (a, b), [P, PASS], U8) for b in range(2)] for a in range(2)]
        tab = [tile("tab%d" % a, [P, T], U32) for a in range(2)]
        tab_sc = tile("tab_sc", [P, T], U8)
        w2_raw = tile("w2_raw", [P, 4 * N], U8)
        w2_sc_raw = tile("w2_sc_raw", [P, N], U8)
        w2_sc = {1: tile("w2_sc1", [P, N], U8)}
        gain_t = tile("gain_t", [P, 8], F32)
        freq_t = tile("freq_t", [P, 8], F32)
        amp_t = tile("amp_t", [P, 8], F32)
        ident = tile("ident", [P, P], F32)
        wgs_raw = tile("wgs_raw", [P, S], F32)
        wgs_turned = [tile("wgs_turned0", [P, S], F32)[:]]
        wgs_t = [tile("wgs%d" % i, [P, S], F32)[:] for i in range(PACK - 1)]
        wgt_t = tile("wgt_t", [P, M], F32)
        pages = [tile("page%d" % u, [P, T2], F32) for u in range(7)]
        h = [tile("h%d" % u, [P, S], F32) for u in range(8)]
        x_wide = [tile("x_wide%d" % n, [P, M], F32) for n in range(2)]
        ripple = tile("ripple", [P, 2 * M], F32)
        z_turned = [tile("z_turned%d" % c, [P, PASS], BF16) for c in range(4)]
        z_rows = tile("z_rows", [P, PACK * M], BF16)
        z_bf = [tile("z_bf%d" % b, [P, PACK * M], BF16) for b in range(2)]
        z_codes = [tile("z_codes%d" % b, [P, M], U32) for b in range(2)]
        z_scale = [tile("z_scale%d" % b, [P, M], U8) for b in range(2)]
        y = [[tile("y%d%d" % (c, g), [P, PACK * w], F32) for g in range(2)] for c, w in enumerate(CHUNKS)]
        y_bf = [[tile("y_bf%d%d" % (c, g), [P, PACK * w], BF16) for g in range(2)] for c, w in enumerate(CHUNKS)]
        y_codes = tile("y_codes", [P, 2 * M], U32)
        y_scale = tile("y_scale", [P, 2 * M], U8)

        def load_w1(a, b):
            rows = w1[a * PASS : (a + 1) * PASS, b * PASS : (b + 1) * PASS]
            nc.sync.dma_start(out=w1_raw[a][b][:], in_=rows.rearrange("(p j) c -> p j c", j=PACK))

        def load_tab(a):
            nc.sync.dma_start(out=tab[a][:].bitcast(I32), in_=tab_words[a].rearrange("p t i -> p (t i)").bitcast(I32))

        def load_page(u):
            b, i = divmod(u, PACK)
            nc.sync.dma_start(out=pages[u][:], in_=page0.rearrange("(b p i) c -> b i p c", b=2, i=PACK)[b, i])

        def load_rows(dst, src):
            nc.sync.dma_start(
                out=dst[:].rearrange("p (b i) -> p b i", b=2), in_=src.rearrange("(b p i) -> p b i", b=2, i=PACK)
            )

        def load_scale_rows(queue, dst, src):
            for q in range(4):
                queue.dma_start(
                    out=dst[32 * q : 32 * q + 8, :].bitcast(I32), in_=src[:, 4 * q : 4 * q + 4, :].bitcast(I32)
                )

        make_identity(nc, ident[:])
        nc.vector.memset(tab_sc[:].bitcast(I32), 0)
        load_scale_rows(nc.gpsimd, tab_sc, tab_scales)
        nc.vector.memset(w2_sc_raw[:].bitcast(I32), 0)
        nc.vector.memset(w2_sc[1][:].bitcast(I32), 0)
        nc.sync.dma_start(out=wgs_raw[:], in_=wgs)
        load_w1(0, 0)
        nc.sync.dma_start(list1[:], offs)
        nc.sync.dma_start(list2[:], offs2)
        load_w1(1, 0)
        load_tab(0)
        load_tab(1)
        nc.sync.dma_start(
            out=w2_raw[:].bitcast(I32).rearrange("p (b c) -> p b c", b=2),
            in_=w2_words.bitcast(I32).rearrange("b p c -> p b c"),
        )
        load_rows(gain_t, gain)
        load_page(0)
        nc.sync.dma_start(out=wgt_t[:], in_=wgt)
        nc.sync.dma_start(list3[:], offs3)
        load_rows(freq_t, freq)
        load_page(1)
        load_rows(amp_t, amp)
        load_w1(0, 1)
        load_w1(1, 1)
        load_page(2)
        load_scale_rows(nc.sync, w2_sc_raw, w2_scales)
        for u in range(3, 7):
            load_page(u)

        def repeat_wgs(i):
            turned = banks[3][:].rearrange("j (c q i) -> j i c q", c=4, i=PACK)[:, i]
            nc.scalar.copy(
                out=wgs_turned[i].rearrange("j (c r q) -> j c r q", c=4, r=4),
                in_=turned.unsqueeze(2).to_broadcast([P, 4, 4, 32]),
            )

        def turn_wgs(i, bank):
            for c in range(4):
                cols = slice(c * P, (c + 1) * P)
                nc.tensor.transpose(bank[:, cols], wgs_turned[i][:, cols], ident[:])
            nc.scalar.copy(out=wgs_t[i], in_=bank[:])

        def cast_w1(copy, a, b, m0, m1):
            copy(
                out=w1_bf[a][b][:].rearrange("p (i m j) -> p m i j", i=PACK, j=PACK)[:, m0:m1],
                in_=w1_raw[a][b][:].rearrange("p j (m i) -> p m i j", i=PACK)[:, m0:m1],
            )

        def quantize(codes, scale, values):
            nc.vector.quantize_mx(out=codes.bitcast(FP8X4), scales=scale, in_=values)

        def quantize_w1(a, b):
            quantize(w1_codes[a, b], w1_scale[a][b][:], w1_bf[a][b][:])

        def deal(dst, src):
            nc.vector.tensor_copy(
                out=dst.rearrange("p (a t mb mi) -> p a mb t mi", t=PACK, mb=16, mi=8),
                in_=src.rearrange("p (a mb mi t) -> p a mb t mi", t=PACK, mb=16, mi=8),
            )

        def first_product(u):
            b, i = divmod(u, PACK)
            cols = slice(i * P, (i + 1) * P)
            order = (0, 1) if u == 0 or b == 1 else (1, 0)
            for a in order:
                nc.tensor.matmul_mx(
                    out=banks[i][:],
                    lhsT=w1_codes[a, b][:, cols].bitcast(FP8X4),
                    lhsT_scale=w1_scale[a][b][:, cols],
                    rhs=v[a][:].bitcast(FP8X4),
                    rhs_scale=v_sc[4 * a : P, :],
                    start=(a == order[0]),
                    stop=(a == order[1]),
                )
            nc.scalar.activation(out=h[u][:], in_=banks[i][:], func=COPY, scale=gain_t[:, u : u + 1])

        def place(u):
            nc.vector.tensor_tensor(pages[u][:].indirect(list2[:]), h[u][:], wgs_t[u % PACK], MULT)

        def pick(u, m0, w, x, s):
            offsets = list3[:, m0 // 16 : (m0 + w) // 16]
            nc.vector.tensor_tensor(x, pages[u][:].indirect(offsets), wgt_t[:, m0 : m0 + w], MULT)
            nc.scalar.activation(out=s, in_=x, func=SIN, scale=freq_t[:, u : u + 1])

        def add_turned(u, x, s):
            nc.scalar.activation(out=s, in_=s, func=COPY, scale=amp_t[:, u : u + 1])
            for c in range(4):
                cols = slice(c * P, (c + 1) * P)
                for term, first in ((x, True), (s, False)):
                    nc.tensor.matmul(
                        banks[4 + c][:, u * P : (u + 1) * P], term[:, cols], ident[:],
                        start=first, stop=not first, is_transpose=True,
                    )

        def turn_back(c):
            nc.scalar.copy(
                out=z_turned[c][:].rearrange("m (p i) -> m p i", i=PACK),
                in_=banks[4 + c][:].rearrange("m (i p) -> m p i", i=PACK),
            )
            pairs = z_turned[c][:].bitcast(F32)
            for e in range(2):
                nc.tensor.transpose(banks[4 + c][:, e * P : (e + 1) * P], pairs[:, e : 2 * P : 2], ident[:])
            nc.scalar.copy(
                out=z_bf[0][:, c * PASS : (c + 1) * PASS].bitcast(F32).rearrange("p (m e) -> p m e", e=2),
                in_=banks[4 + c][:, 0 : 2 * P].rearrange("p (e m) -> p m e", e=2),
            )

        def interleave(copy, dst, src):
            copy(
                out=dst.rearrange("p (c i t) -> p c t i", i=4, t=PACK),
                in_=src.rearrange("p (t c i) -> p c t i", i=4, t=PACK),
            )

        starts = [sum(CHUNKS[:c]) for c in range(len(CHUNKS))]
        chunk_banks = [banks[m0 // 64 : (m0 + w) // 64] for m0, w in zip(starts, CHUNKS)]
        last = len(CHUNKS) - 1

        def second_product(b, c):
            m0, w = starts[c], CHUNKS[c]
            per_bank = BANK // w
            for n in range(8):
                slot = n % per_bank
                nc.tensor.matmul_mx(
                    out=chunk_banks[c][n // per_bank][:, slot * w : (slot + 1) * w],
                    lhsT=w2_dealt[:, 2 * (b * N + n * P) : 2 * (b * N + (n + 1) * P)].bitcast(FP4X4),
                    lhsT_scale=w2_sc[b][:, n * P : (n + 1) * P],
                    rhs=z_codes[b][:, m0 : m0 + w].bitcast(FP8X4),
                    rhs_scale=z_scale[b][:, m0 : m0 + w],
                    start=(b == 0 and slot == 0),
                    stop=(b == 1 and slot == per_bank - 1),
                )

        def take_out(c, g):
            m0, w = starts[c], CHUNKS[c]
            per_group = len(chunk_banks[c]) // 2
            copy = nc.vector.tensor_copy if (c == last and g == 1) else nc.scalar.copy
            for n in range(per_group):
                copy(out=y[c][g][:, n * BANK : (n + 1) * BANK], in_=chunk_banks[c][g * per_group + n][:])
            nc.sync.dma_start(
                out=out_0.rearrange("(g p t) m -> g p t m", g=2, t=PACK)[g, :, :, m0 : m0 + w],
                in_=y[c][g][:].rearrange("p (t m) -> p t m", t=PACK),
            )
            interleave(nc.vector.tensor_copy if (g == 1 or c == 0) else nc.scalar.copy, y_bf[c][g][:], y[c][g][:])

        def planes(c):
            m0, w = starts[c], CHUNKS[c]
            for g in range(2):
                cols = slice(g * M + m0, g * M + m0 + w)
                quantize(y_codes[:, cols], y_scale[:, cols], y_bf[c][g][:])
            nc.sync.dma_start(
                out=out_1.rearrange("g p m t -> p g (m t)").bitcast(I32)[:, :, m0 : m0 + w],
                in_=y_codes[:].bitcast(I32).rearrange("p (g m) -> p g m", g=2)[:, :, m0 : m0 + w],
            )

        for c in range(4):
            cols = slice(c * P, (c + 1) * P)
            nc.tensor.transpose(banks[3][:, cols], wgs_raw[:, cols], ident[:])
        repeat_wgs(0)
        turn_wgs(0, banks[4])
        for a in range(2):
            cast_w1(nc.vector.tensor_copy, a, 0, 0, CAST_SPLIT)
            cast_w1(nc.scalar.copy, a, 0, CAST_SPLIT, P)
            quantize_w1(a, 0)
        v = [tile("v0", [P, S], U32, tag="w1_bf10")]
        nc.vector.tensor_copy(v[0][:], tab[0][:].indirect(list1[:]))
        v_sc = tile("v_sc", [P, S], U8, tag="tab0")
        nc.vector.tensor_copy(v_sc[:], tab_sc[:].indirect(list1[:]))
        v.append(tile("v1", [P, S], U32, tag="tab_sc"))
        nc.vector.tensor_copy(v[1][:], tab[1][:].indirect(list1[:]))
        w2_dealt = tile("w2_dealt", [P, 4 * N], U8, tag="tab1")
        deal(w2_dealt[:].bitcast(U16), w2_raw[:].bitcast(U16))
        first_product(0)
        turned_rest = tile("turned_rest", [P, 3 * S], F32, tag="w1_raw10")
        for i in range(1, PACK):
            wgs_turned.append(turned_rest[:, (i - 1) * S : i * S])
            repeat_wgs(i)
        for u in range(1, PACK):
            first_product(u)
            if u < PACK - 1:
                turn_wgs(u, banks[u - 1])

        for u in range(PACK):
            if u == 1:
                cast_w1(nc.scalar.copy, 0, 1, 0, P)
                cast_w1(nc.scalar.copy, 1, 1, 0, P)
                after_cast = tile("after_cast", [P, M + S], F32, tag="w1_raw11")
                wgs_t.append(after_cast[:, M : M + S])
                turn_wgs(PACK - 1, banks[2])
            place(u)
            x = x_wide[u % 2][:]
            s = after_cast[:, 0:M] if u % 2 else ripple[:, 0:M]
            pick(u, 0, M, x, s)
            add_turned(u, x, s)
            if u == 2:
                late_codes = tile("late_codes", [P, 2 * PASS], U32, tag="h2")
                for a in range(2):
                    w1_codes[a, 1] = late_codes[:, a * PASS : (a + 1) * PASS]
                    quantize_w1(a, 1)
                for later in range(PACK, 2 * PACK):
                    first_product(later)
        w2_sc[0] = tile("w2_sc0", [P, N], U8, tag="h3")
        deal(w2_sc[0][:], w2_sc_raw[:])
        for q in range(4):
            nc.sync.dma_start(
                out=w2_sc[1][32 * q : 32 * q + 4, :].bitcast(I32), in_=w2_sc[0][32 * q + 4 : 32 * q + 8, :].bitcast(I32)
            )
        for c in range(4):
            turn_back(c)
        pages.append(tile("page7", [P, T2], F32, tag="z_turned0"))
        load_page(7)
        for u in range(PACK, 7):
            place(u)
        quantize(z_codes[0][:], z_scale[0][:], z_bf[0][:])
        for c in range(len(CHUNKS)):
            second_product(0, c)
        place(7)

        steps = [(c, u) for c in range(len(CHUNKS)) for u in range(PACK, 2 * PACK)]
        x_ring = [h[7][:, 0:256], h[7][:, 256:512], wgs_t[3][:, 0:256], wgs_t[3][:, 256:512]]

        def buffers(k):
            w = CHUNKS[steps[k][0]]
            slot = k % RING
            return x_ring[slot][:, 0:w], ripple[:, slot * 256 : slot * 256 + w]

        def combine(k):
            c, u = steps[k]
            m0, w = starts[c], CHUNKS[c]
            i = u - PACK
            x, s = buffers(k)
            rows = z_rows[:, PACK * m0 : PACK * (m0 + w)]
            nc.vector.scalar_tensor_tensor(
                out=rows[:, i * w : (i + 1) * w], in0=s, scalar=amp_t[:, u : u + 1], in1=x, op0=MULT, op1=ADD
            )
            if i == PACK - 1:
                copy = nc.vector.tensor_copy if c == last else nc.scalar.copy
                interleave(copy, z_bf[1][:, PACK * m0 : PACK * (m0 + w)], rows)

        for k in range(len(steps) + 8):
            if k < len(steps):
                c, u = steps[k]
                pick(u, starts[c], CHUNKS[c], *buffers(k))
            if 0 <= k - 1 < len(steps):
                combine(k - 1)
            if 0 <= k - 3 < len(steps) and (k - 3) % PACK == PACK - 1:
                c = steps[k - 3][0]
                m0, w = starts[c], CHUNKS[c]
                quantize(z_codes[1][:, m0 : m0 + w], z_scale[1][:, m0 : m0 + w], z_bf[1][:, PACK * m0 : PACK * (m0 + w)])
                second_product(1, c)
                take_out(c, 0)
                take_out(c, 1)
            if 0 <= k - 6 < len(steps) and (k - 6) % PACK == PACK - 1:
                planes(steps[k - 6][0])

        for q in range(4):
            queue = nc.sync if q % 2 == 0 else nc.scalar
            queue.dma_start(
                out=out_2[:, 4 * q : 4 * q + 4, :].bitcast(I32).rearrange("g r m -> r g m"),
                in_=y_scale[32 * q : 32 * q + 4, :].bitcast(I32).rearrange("r (g m) -> r g m", g=2),
            )
